import numpy as np
import ml_dtypes

BF16 = ml_dtypes.bfloat16


def bf(x):
    return np.asarray(x, np.float32).astype(BF16)


def f32(x):
    return np.asarray(x, np.float32)


def f64(x):
    return np.asarray(x).astype(np.float64)


def striped(idx):
    return np.tile(idx.reshape(-1, 16).T, (8, 1))


def rows(idx, k):
    return np.tile(idx, (k, 1))


def look(tab, idx):
    return np.take_along_axis(f64(tab), rows(idx, len(tab)), axis=1)


K, S, V, N, M = 128, 2048, 2048, 2048, 512


def setup_inputs():
    return {"tab": f32(np.random.standard_normal((2, K, S))), "y": f32(np.random.standard_normal((K, V))), "w": bf(np.random.standard_normal((K, M)) / np.sqrt(K)), "b": f32(0.5 * np.random.standard_normal((M, 1))), "offs": striped(np.random.permutation(S)[:N])}


def reference(tab, y, w, b, offs):
    idx = offs[:16].T.reshape(-1)
    x = (look(tab[0], idx) + f64(y)) * (np.maximum(look(tab[1], idx), 0.0))
    return np.maximum(f64(w).T @ x + f64(b), 0.0)

@@ -1,0 +1,62 @@
+import concourse.mybir as mybir
+
+BF16, F32, U16 = mybir.dt.bfloat16, mybir.dt.float32, mybir.dt.uint16
+add, mult, maximum = mybir.AluOpType.add, mybir.AluOpType.mult, mybir.AluOpType.max
+relu = mybir.ActivationFunctionType.Relu
+
+P = 128
+PLACES = 2048
+N = 2048
+M = 512
+PIECE = 512
+BLOCKS = M // P
+FLOPS = 2 * P * M * N
+
+
+def tile_lookup_vg_addrelu_relu_kernel(tc, tab, y, w, b, offs, out):
+    nc = tc.nc
+    out_rows = out.rearrange("(p c) i -> p c i", c=BLOCKS)
+    b_rows = b.rearrange("(p c) one -> p (c one)", c=BLOCKS)
+    with (
+        tc.tile_pool(name="held", bufs=1) as held,
+        tc.tile_pool(name="work", bufs=2) as work,
+        tc.tile_pool(name="results", bufs=4) as results,
+        tc.psum_pool(name="banks", bufs=8) as banks,
+    ):
+        offsets = held.tile([P, N // 16], U16, name="offsets")
+        values = held.tile([P, PLACES], F32, name="values")
+        gates = held.tile([P, PLACES], F32, name="gates")
+        stream = held.tile([P, N], F32, name="stream")
+        weights = held.tile([P, M], BF16, name="weights")
+        biases = held.tile([P, BLOCKS], F32, name="biases")
+
+        nc.sync.dma_start(offsets[:], offs)
+        nc.sync.dma_start(values[:], tab[0])
+        nc.sync.dma_start(stream[:, 0:PIECE], y[:, 0:PIECE])
+        nc.sync.dma_start(gates[:], tab[1])
+        nc.sync.dma_start(weights[:], w)
+        nc.sync.dma_start(biases[:], b_rows)
+        nc.sync.dma_start(stream[:, PIECE:N], y[:, PIECE:N])
+        weights_of = weights[:].rearrange("r (p c) -> r c p", c=BLOCKS)
+
+        for first in range(0, N, PIECE):
+            piece = slice(first, first + PIECE)
+            entries = offsets[:, first // 16 : (first + PIECE) // 16]
+
+            summed = work.tile([P, PIECE], F32, name="summed")
+            opened = work.tile([P, PIECE], F32, name="opened")
+            x = work.tile([P, PIECE], BF16, name="x")
+            nc.vector.tensor_tensor(summed[:], values[:].indirect(entries), stream[:, piece], add)
+            nc.scalar.activation(opened[:], gates[:].indirect(entries), relu)
+            nc.vector.tensor_tensor(x[:], summed[:], opened[:], mult)
+
+            for even in range(0, BLOCKS, 2):
+                odd = even + 1
+                result = results.tile([P, 2, PIECE], F32, name="result")
+                product_even = banks.tile([P, PIECE], F32, name="product", tag="product")
+                nc.tensor.matmul(product_even[:], weights_of[:, even, :], x[:], start=True, stop=True)
+                product_odd = banks.tile([P, PIECE], F32, name="product", tag="product")
+                nc.tensor.matmul(product_odd[:], weights_of[:, odd, :], x[:], start=True, stop=True)
+                nc.scalar.activation(result[:, 0, :], product_even[:], relu, bias=biases[:, even : even + 1])
+                nc.vector.tensor_scalar(result[:, 1, :], product_odd[:], biases[:, odd : odd + 1], 0.0, add, maximum)
+                nc.sync.dma_start(out_rows[:, even : even + 2, piece], result[:])

@@ -8,7 +8,7 @@ P = 128
 PLACES = 2048
 N = 2048
 M = 512
-PIECE = 512
+PIECE = 256
 BLOCKS = M // P
 FLOPS = 2 * P * M * N
 
@@ -19,8 +19,8 @@ def tile_lookup_vg_addrelu_relu_kernel(tc, tab, y, w, b, offs, out):
     b_rows = b.rearrange("(p c) one -> p (c one)", c=BLOCKS)
     with (
         tc.tile_pool(name="held", bufs=1) as held,
-        tc.tile_pool(name="work", bufs=2) as work,
-        tc.tile_pool(name="results", bufs=4) as results,
+        tc.tile_pool(name="work", bufs=N // PIECE) as work,
+        tc.tile_pool(name="results", bufs=N // PIECE) as results,
         tc.psum_pool(name="banks", bufs=8) as banks,
     ):
         offsets = held.tile([P, N // 16], U16, name="offsets")
@@ -31,32 +31,32 @@ def tile_lookup_vg_addrelu_relu_kernel(tc, tab, y, w, b, offs, out):
         biases = held.tile([P, BLOCKS], F32, name="biases")
 
         nc.sync.dma_start(offsets[:], offs)
-        nc.sync.dma_start(values[:], tab[0])
-        nc.sync.dma_start(stream[:, 0:PIECE], y[:, 0:PIECE])
         nc.sync.dma_start(gates[:], tab[1])
-        nc.sync.dma_start(weights[:], w)
-        nc.sync.dma_start(biases[:], b_rows)
-        nc.sync.dma_start(stream[:, PIECE:N], y[:, PIECE:N])
+        nc.scalar.dma_start(weights[:], w)
+        nc.scalar.dma_start(biases[:], b_rows)
+        nc.sync.dma_start(values[:], tab[0])
+        for first in range(0, N, PIECE):
+            nc.sync.dma_start(stream[:, first : first + PIECE], y[:, first : first + PIECE])
         weights_of = weights[:].rearrange("r (p c) -> r c p", c=BLOCKS)
 
         for first in range(0, N, PIECE):
             piece = slice(first, first + PIECE)
             entries = offsets[:, first // 16 : (first + PIECE) // 16]
 
-            summed = work.tile([P, PIECE], F32, name="summed")
             opened = work.tile([P, PIECE], F32, name="opened")
+            summed = work.tile([P, PIECE], F32, name="summed")
             x = work.tile([P, PIECE], BF16, name="x")
-            nc.vector.tensor_tensor(summed[:], values[:].indirect(entries), stream[:, piece], add)
             nc.scalar.activation(opened[:], gates[:].indirect(entries), relu)
+            nc.vector.tensor_tensor(summed[:], values[:].indirect(entries), stream[:, piece], add)
             nc.vector.tensor_tensor(x[:], summed[:], opened[:], mult)
 
-            for even in range(0, BLOCKS, 2):
-                odd = even + 1
-                result = results.tile([P, 2, PIECE], F32, name="result")
-                product_even = banks.tile([P, PIECE], F32, name="product", tag="product")
-                nc.tensor.matmul(product_even[:], weights_of[:, even, :], x[:], start=True, stop=True)
-                product_odd = banks.tile([P, PIECE], F32, name="product", tag="product")
-                nc.tensor.matmul(product_odd[:], weights_of[:, odd, :], x[:], start=True, stop=True)
-                nc.scalar.activation(result[:, 0, :], product_even[:], relu, bias=biases[:, even : even + 1])
-                nc.vector.tensor_scalar(result[:, 1, :], product_odd[:], biases[:, odd : odd + 1], 0.0, add, maximum)
-                nc.sync.dma_start(out_rows[:, even : even + 2, piece], result[:])
+            result = results.tile([P, BLOCKS, PIECE], F32, name="result")
+            for c in range(BLOCKS):
+                product = banks.tile([P, PIECE], F32, name="product")
+                nc.tensor.matmul(product[:], weights_of[:, c, :], x[:], start=True, stop=True)
+                if c == 1:
+                    nc.vector.tensor_scalar(result[:, c, :], product[:], biases[:, c : c + 1], 0.0, add, maximum)
+                else:
+                    nc.scalar.activation(result[:, c, :], product[:], relu, bias=biases[:, c : c + 1])
+                if c % 2 == 1:
+                    nc.sync.dma_start(out_rows[:, c - 1 : c + 1, piece], result[:, c - 1 : c + 1, :])

@@ -8,7 +8,7 @@ P = 128
 PLACES = 2048
 N = 2048
 M = 512
-PIECE = 256
+SHORT, LONG = 256, 512
 BLOCKS = M // P
 FLOPS = 2 * P * M * N
 
@@ -19,8 +19,10 @@ def tile_lookup_vg_addrelu_relu_kernel(tc, tab, y, w, b, offs, out):
     b_rows = b.rearrange("(p c) one -> p (c one)", c=BLOCKS)
     with (
         tc.tile_pool(name="held", bufs=1) as held,
-        tc.tile_pool(name="work", bufs=N // PIECE) as work,
-        tc.tile_pool(name="results", bufs=N // PIECE) as results,
+        tc.tile_pool(name="opened", bufs=3) as opened_pool,
+        tc.tile_pool(name="summed", bufs=2) as summed_pool,
+        tc.tile_pool(name="x", bufs=3) as x_pool,
+        tc.tile_pool(name="results", bufs=5) as results,
         tc.psum_pool(name="banks", bufs=8) as banks,
     ):
         offsets = held.tile([P, N // 16], U16, name="offsets")
@@ -35,24 +37,26 @@ def tile_lookup_vg_addrelu_relu_kernel(tc, tab, y, w, b, offs, out):
         nc.scalar.dma_start(weights[:], w)
         nc.scalar.dma_start(biases[:], b_rows)
         nc.sync.dma_start(values[:], tab[0])
-        for first in range(0, N, PIECE):
-            nc.sync.dma_start(stream[:, first : first + PIECE], y[:, first : first + PIECE])
+        for first in range(0, N, 512):
+            nc.sync.dma_start(stream[:, first : first + 512], y[:, first : first + 512])
         weights_of = weights[:].rearrange("r (p c) -> r c p", c=BLOCKS)
 
-        for first in range(0, N, PIECE):
-            piece = slice(first, first + PIECE)
-            entries = offsets[:, first // 16 : (first + PIECE) // 16]
+        first = 0
+        while first < N:
+            length = min(max(first, SHORT), LONG)
+            piece = slice(first, first + length)
+            entries = offsets[:, first // 16 : (first + length) // 16]
 
-            opened = work.tile([P, PIECE], F32, name="opened")
-            summed = work.tile([P, PIECE], F32, name="summed")
-            x = work.tile([P, PIECE], BF16, name="x")
+            opened = opened_pool.tile([P, length], F32, name="opened")
+            summed = summed_pool.tile([P, length], F32, name="summed")
+            x = x_pool.tile([P, length], BF16, name="x")
             nc.scalar.activation(opened[:], gates[:].indirect(entries), relu)
             nc.vector.tensor_tensor(summed[:], values[:].indirect(entries), stream[:, piece], add)
             nc.vector.tensor_tensor(x[:], summed[:], opened[:], mult)
 
-            result = results.tile([P, BLOCKS, PIECE], F32, name="result")
+            result = results.tile([P, BLOCKS, length], F32, name="result")
             for c in range(BLOCKS):
-                product = banks.tile([P, PIECE], F32, name="product")
+                product = banks.tile([P, length], F32, name="product")
                 nc.tensor.matmul(product[:], weights_of[:, c, :], x[:], start=True, stop=True)
                 if c == 1:
                     nc.vector.tensor_scalar(result[:, c, :], product[:], biases[:, c : c + 1], 0.0, add, maximum)
@@ -60,3 +64,4 @@ def tile_lookup_vg_addrelu_relu_kernel(tc, tab, y, w, b, offs, out):
                     nc.scalar.activation(result[:, c, :], product[:], relu, bias=biases[:, c : c + 1])
                 if c % 2 == 1:
                     nc.sync.dma_start(out_rows[:, c - 1 : c + 1, piece], result[:, c - 1 : c + 1, :])
+            first += length

import concourse.mybir as mybir

BF16, F32, U16 = mybir.dt.bfloat16, mybir.dt.float32, mybir.dt.uint16
add, mult, maximum = mybir.AluOpType.add, mybir.AluOpType.mult, mybir.AluOpType.max
relu = mybir.ActivationFunctionType.Relu

P = 128
PLACES = 2048
N = 2048
M = 512
SHORT, LONG = 256, 512
BLOCKS = M // P
FLOPS = 2 * P * M * N


def tile_lookup_vg_addrelu_relu_kernel(tc, tab, y, w, b, offs, out):
    nc = tc.nc
    out_rows = out.rearrange("(p c) i -> p c i", c=BLOCKS)
    b_rows = b.rearrange("(p c) one -> p (c one)", c=BLOCKS)
    with (
        tc.tile_pool(name="held", bufs=1) as held,
        tc.tile_pool(name="opened", bufs=3) as opened_pool,
        tc.tile_pool(name="summed", bufs=2) as summed_pool,
        tc.tile_pool(name="x", bufs=3) as x_pool,
        tc.tile_pool(name="results", bufs=5) as results,
        tc.psum_pool(name="banks", bufs=8) as banks,
    ):
        offsets = held.tile([P, N // 16], U16, name="offsets")
        values = held.tile([P, PLACES], F32, name="values")
        gates = held.tile([P, PLACES], F32, name="gates")
        stream = held.tile([P, N], F32, name="stream")
        weights = held.tile([P, M], BF16, name="weights")
        biases = held.tile([P, BLOCKS], F32, name="biases")

        nc.sync.dma_start(offsets[:], offs)
        nc.sync.dma_start(gates[:], tab[1])
        nc.scalar.dma_start(weights[:], w)
        nc.scalar.dma_start(biases[:], b_rows)
        nc.sync.dma_start(values[:], tab[0])
        for first in range(0, N, 512):
            nc.sync.dma_start(stream[:, first : first + 512], y[:, first : first + 512])
        weights_of = weights[:].rearrange("r (p c) -> r c p", c=BLOCKS)

        first = 0
        while first < N:
            length = min(max(first, SHORT), LONG)
            piece = slice(first, first + length)
            entries = offsets[:, first // 16 : (first + length) // 16]

            opened = opened_pool.tile([P, length], F32, name="opened")
            summed = summed_pool.tile([P, length], F32, name="summed")
            x = x_pool.tile([P, length], BF16, name="x")
            nc.scalar.activation(opened[:], gates[:].indirect(entries), relu)
            nc.vector.tensor_tensor(summed[:], values[:].indirect(entries), stream[:, piece], add)
            nc.vector.tensor_tensor(x[:], summed[:], opened[:], mult)

            result = results.tile([P, BLOCKS, length], F32, name="result")
            for c in range(BLOCKS):
                product = banks.tile([P, length], F32, name="product")
                nc.tensor.matmul(product[:], weights_of[:, c, :], x[:], start=True, stop=True)
                if c == 1:
                    nc.vector.tensor_scalar(result[:, c, :], product[:], biases[:, c : c + 1], 0.0, add, maximum)
                else:
                    nc.scalar.activation(result[:, c, :], product[:], relu, bias=biases[:, c : c + 1])
                if c % 2 == 1:
                    nc.sync.dma_start(out_rows[:, c - 1 : c + 1, piece], result[:, c - 1 : c + 1, :])
            first += length
